import numpy as np
import ml_dtypes


def mxq(x, axis, fmt="e4m3"):
    dtype, down = {"e4m3": (ml_dtypes.float8_e4m3fn, 7), "e5m2": (ml_dtypes.float8_e5m2, 14)}[fmt]
    v = np.moveaxis(np.asarray(x, np.float32).astype(ml_dtypes.bfloat16).astype(np.float64), axis, -1)
    blocks = v.reshape(v.shape[:-1] + (-1, 32))
    amax = np.abs(blocks).max(-1, keepdims=True)
    byte = np.maximum(np.where(amax > 0, np.frexp(amax)[1] - 1 + 127, 0) - down, 1)
    scale = np.exp2(byte - 127.0)
    codes = (blocks / scale).astype(np.float32).astype(dtype).astype(np.float64)
    return np.moveaxis((codes * scale).reshape(v.shape), -1, axis)


WIDE = False


def mx_kscale(k):
    if not WIDE:
        return np.ones(k)
    levels = np.array([10, -10, 5, -5, 0])
    if k % 512:
        return np.exp2(np.random.permutation(np.resize(levels, k // 32))).repeat(32)
    a = np.empty((k // 512, 16))
    for p in range(k // 512):
        a[p, :8] = np.random.permutation(np.resize(levels, 8))
        for g in range(8):
            far = levels[np.abs(levels - a[p, g]) >= 10]
            a[p, g + 8] = far[np.random.randint(len(far))]
    return np.exp2(a.ravel()).repeat(32)


def f64(x):
    return np.asarray(x).astype(np.float64)


def striped(idx):
    return np.tile(np.asarray(idx).reshape(-1, 16).T, (8, 1)).astype(np.uint16)


def unstriped(offs):
    return offs[:16].T.reshape(-1).astype(np.int64)


E2M1 = np.array([0.0, 0.5, 1.0, 1.5, 2.0, 3.0, 4.0, 6.0, -0.0, -0.5, -1.0, -1.5, -2.0, -3.0, -4.0, -6.0])


def pack_weight(w, fmt):
    k, n = w.shape
    w = f64(np.asarray(w, np.float32).astype(ml_dtypes.bfloat16)).reshape(k // 32, 32, n)
    amax = np.abs(w).max(1)
    if fmt == "e4m3":
        byte = np.frexp(amax)[1] - 1 + 127 - 7
    else:
        mant, ex = np.frexp(amax / 6.0)
        byte = np.where(mant > 0.5, ex, ex - 1) + 127
    byte = np.clip(np.where(amax > 0, byte, 1), 1, 254)
    scaled = (w * np.exp2(127.0 - byte)[:, None, :]).reshape(k, n).astype(np.float32)
    by_word = np.ascontiguousarray(scaled.reshape(k // 512, 128, 4, n).transpose(0, 1, 3, 2))
    if fmt == "e4m3":
        words = by_word.astype(ml_dtypes.float8_e4m3fn).view(np.uint8)
    else:
        c = by_word.astype(ml_dtypes.float4_e2m1fn).view(np.uint8) & 0xF
        words = (c[..., 0::2] | (c[..., 1::2] << 4)).reshape(k // 512, 128, 2 * n)
    return np.ascontiguousarray(words), np.ascontiguousarray(byte.astype(np.uint8).reshape(k // 512, 16, n))


def unpack_weight(words, scales, fmt):
    g, _, n = scales.shape
    words = np.ascontiguousarray(words).reshape(g, 128, n, -1)
    if fmt == "e4m3":
        vals = words.view(ml_dtypes.float8_e4m3fn).astype(np.float64)
    else:
        nib = np.empty((g, 128, n, 4), np.uint8)
        nib[..., 0::2] = words & 0xF
        nib[..., 1::2] = words >> 4
        vals = E2M1[nib]
    vals = vals * np.repeat(np.exp2(scales.astype(np.float64) - 127.0), 8, axis=1)[..., None]
    return vals.transpose(0, 1, 3, 2).reshape(g * 512, n)


def sigmoid(v):
    return 1.0 / (1.0 + np.exp(-v))


K, R, F, T, J, G = 512, 128, 512, 2048, 512, 64


def setup_inputs():
    n = np.random.standard_normal
    idx = np.random.permutation(T)[:J]
    fk = mx_kscale(K)
    ff = mx_kscale(F)
    tabp = pack_weight(n((K, T)) / fk[:, None], "e4m3")
    return {
        "tab_words": tabp[0],
        "tab_scales": tabp[1],
        "w1": (n((K, R)) * 1 / np.sqrt(K) * fk[:, None]).astype(np.float32),
        "steep": (np.random.uniform(1.0, 4.0, (R, 1))).astype(np.float32),
        "wo": (n((F, R)) * 1 / np.sqrt(F) * ff[:, None]).astype(np.float32),
        "dy": (n((F, G)) / ff[:, None]).astype(np.float32),
        "old": (0.5 * n((R, J))).astype(np.float32),
        "offs": striped(idx),
    }


def reference(tab_words, tab_scales, w1, steep, wo, dy, old, offs):
    idx = unstriped(offs)
    tabu = unpack_weight(tab_words, tab_scales, "e4m3")
    w1q = mxq(f64(w1), 0, "e4m3")
    tabidxg = tabu[:, idx]
    a = w1q.T @ tabidxg
    h1 = np.tanh(a)
    p = sigmoid(a * f64(steep))
    z = p.reshape(R, G, J // G).sum(axis=2)
    woq = mxq(f64(wo), 0, "e4m3")
    dyq = mxq(f64(dy), 0, "e4m3")
    c0 = woq.T @ dyq
    e1 = c0 / z
    r1 = np.repeat(e1, J // G, axis=1)
    dz = c0 * (p * h1).reshape(R, G, J // G).sum(axis=2) / np.square(z) * (-1.0)
    r2 = np.repeat(dz, J // G, axis=1)
    dp = r1 * h1 + r2
    dh1 = r1 * p
    da = dp * p * (1.0 - p) * f64(steep) + dh1 * (1.0 - np.square(h1))
    y = da + f64(old)
    return y

@@ -1,0 +1,167 @@
+from contextlib import ExitStack
+
+import concourse.mybir as mybir
+
+K, R, F, T, J, G = 512, 128, 512, 2048, 512, 64
+FLOPS = 2 * K * R * J + 2 * F * R * G
+
+F32 = mybir.dt.float32
+BF16 = mybir.dt.bfloat16
+I32 = mybir.dt.int32
+U32 = mybir.dt.uint32
+U16 = mybir.dt.uint16
+U8 = mybir.dt.uint8
+FP8X4 = mybir.dt.float8_e4m3fn_x4
+ALU = mybir.AluOpType
+ACT = mybir.ActivationFunctionType
+AXIS_X = mybir.AxisListType.X
+
+P = 128
+PACK = 4
+VOTE = J // G
+HALVES = 2
+JH = J // HALVES
+GH = G // HALVES
+
+
+def tile_attend_cgroupvote_kernel(tc, tab_words, tab_scales, w1, steep, wo, dy, old, offs, out):
+    nc = tc.nc
+    with ExitStack() as ctx:
+        keep = ctx.enter_context(tc.tile_pool(name="keep", bufs=1))
+        stage = ctx.enter_context(tc.tile_pool(name="stage", bufs=4))
+        psum = ctx.enter_context(tc.psum_pool(name="psum", bufs=1))
+
+        offsets = keep.tile([P, J // 16], U16, name="offsets")
+        nc.sync.dma_start(offsets[:], offs)
+
+        def load_rows(queue, rows, name):
+            raw = stage.tile([P, PACK, rows.shape[1]], F32, name=name, tag="raw")
+            queue.dma_start(out=raw[:], in_=rows.rearrange("(p t) w -> p t w", t=PACK))
+            return raw
+
+        def interleave(raw, name):
+            width = raw.shape[2]
+            grouped = keep.tile([P, width, PACK], BF16, name=name, align_bytes=64)
+            nc.scalar.copy(out=grouped[:], in_=raw[:].rearrange("p t w -> p w t"))
+            return grouped
+
+        def quantize(grouped, name):
+            width = grouped.shape[1]
+            codes = keep.tile([P, width], U32, name=name + "_codes", align_bytes=64)
+            scales = keep.tile([P, width], U8, name=name + "_scales", align_bytes=64)
+            nc.vector.quantize_mx(
+                out=codes[:].bitcast(FP8X4), scales=scales[:], in_=grouped[:].rearrange("p w t -> p (w t)")
+            )
+            return codes, scales
+
+        w1_raw = load_rows(nc.sync, w1, "w1_raw")
+        steep_col = keep.tile([P, 1], F32, name="steep_col")
+        nc.sync.dma_start(out=steep_col[:], in_=steep)
+        plane = keep.tile([P, T], U8, name="plane", align_bytes=64)
+        nc.vector.memset(plane[:].bitcast(I32), 0)
+        for q in range(4):
+            nc.sync.dma_start(
+                out=plane[32 * q : 32 * q + 4, :].bitcast(I32), in_=tab_scales[0, 4 * q : 4 * q + 4, :].bitcast(I32)
+            )
+        words = keep.tile([P, T], U32, name="words", align_bytes=64)
+        nc.sync.dma_start(out=words[:].bitcast(I32), in_=tab_words[0].rearrange("p n t -> p (n t)").bitcast(I32))
+        wo_raw = load_rows(nc.sync, wo, "wo_raw")
+
+
+        w1_grouped = interleave(w1_raw, "w1_grouped")
+        dy_raw = load_rows(nc.sync, dy, "dy_raw")
+        w1_codes, w1_scales = quantize(w1_grouped, "w1")
+
+        picked_scales = keep.tile([P, J], U8, name="picked_scales", align_bytes=64)
+        nc.vector.tensor_copy(picked_scales[:], plane[:].indirect(offsets[:]))
+
+        a_banks = []
+        for c in range(HALVES):
+            picked = keep.tile([P, JH], U32, name=f"picked_words{c}", align_bytes=64)
+            nc.vector.tensor_copy(picked[:], words[:].indirect(offsets[:, c * (JH // 16) : (c + 1) * (JH // 16)]))
+            bank = psum.tile([P, JH], F32, name=f"a{c}")
+            nc.tensor.matmul_mx(
+                out=bank[:],
+                lhsT=w1_codes[:].bitcast(FP8X4),
+                lhsT_scale=w1_scales[:],
+                rhs=picked[:].bitcast(FP8X4),
+                rhs_scale=picked_scales[:, c * JH : (c + 1) * JH],
+                start=True,
+                stop=True,
+            )
+            a_banks.append(bank)
+
+        wo_grouped = interleave(wo_raw, "wo_grouped")
+        old_sb = stage.tile([P, J], F32, name="old_sb", tag="raw")
+        dy_grouped = interleave(dy_raw, "dy_grouped")
+        nc.sync.dma_start(out=old_sb[:], in_=old)
+
+        def wide(name):
+            return [keep.tile([P, GH, VOTE], F32, name=f"{name}{c}") for c in range(HALVES)]
+
+        def narrow(name):
+            return [keep.tile([P, GH], F32, name=f"{name}{c}") for c in range(HALVES)]
+
+        def spread(col):
+            return col.unsqueeze(2).to_broadcast([P, GH, VOTE])
+
+        p, h, hh, ph = wide("p"), wide("h"), wide("hh"), wide("ph")
+        z, rz, u, ms, e = narrow("z"), narrow("rz"), narrow("u"), narrow("ms"), narrow("e")
+        t1, t2, t3, t4, t5, y = wide("t1"), wide("t2"), wide("t3"), wide("t4"), wide("t5"), wide("y")
+        halves = range(HALVES)
+
+        for c in halves:
+            a = a_banks[c][:].rearrange("p (g i) -> p g i", i=VOTE)
+            nc.scalar.activation(out=p[c][:], in_=a, func=ACT.Sigmoid, scale=steep_col[:])
+            nc.scalar.activation(out=h[c][:], in_=a, func=ACT.Tanh)
+        for c in halves:
+            nc.scalar.activation(out=hh[c][:], in_=h[c][:], func=ACT.Square)
+
+        wo_codes, wo_scales = quantize(wo_grouped, "wo")
+        dy_codes, dy_scales = quantize(dy_grouped, "dy")
+        c0 = psum.tile([P, G], F32, name="c0")
+        nc.tensor.matmul_mx(
+            out=c0[:],
+            lhsT=wo_codes[:].bitcast(FP8X4),
+            lhsT_scale=wo_scales[:],
+            rhs=dy_codes[:].bitcast(FP8X4),
+            rhs_scale=dy_scales[:],
+            start=True,
+            stop=True,
+        )
+
+        for c in halves:
+            nc.vector.tensor_reduce(out=z[c][:], in_=p[c][:], axis=AXIS_X, op=ALU.add)
+            nc.vector.tensor_tensor(out=ph[c][:], in0=p[c][:], in1=h[c][:], op=ALU.mult)
+            nc.vector.reciprocal(out=rz[c][:], in_=z[c][:])
+            nc.vector.tensor_reduce(out=u[c][:], in_=ph[c][:], axis=AXIS_X, op=ALU.add)
+        for c in halves:
+            nc.vector.scalar_tensor_tensor(
+                out=ms[c][:], in0=u[c][:], scalar=steep_col[:], in1=rz[c][:], op0=ALU.mult, op1=ALU.mult
+            )
+        for c in halves:
+            nc.vector.tensor_tensor(out=e[c][:], in0=c0[:, c * GH : (c + 1) * GH], in1=rz[c][:], op=ALU.mult)
+        for c in halves:
+            nc.vector.scalar_tensor_tensor(
+                out=t1[c][:], in0=h[c][:], scalar=steep_col[:], in1=spread(ms[c][:]), op0=ALU.mult, op1=ALU.subtract
+            )
+        for c in halves:
+            nc.vector.scalar_tensor_tensor(
+                out=t2[c][:], in0=p[c][:], scalar=1.0, in1=t1[c][:], op0=ALU.subtract, op1=ALU.mult
+            )
+        for c in halves:
+            nc.vector.scalar_tensor_tensor(
+                out=t3[c][:], in0=hh[c][:], scalar=1.0, in1=t2[c][:], op0=ALU.subtract, op1=ALU.add
+            )
+        for c in halves:
+            nc.vector.tensor_tensor(out=t4[c][:], in0=t3[c][:], in1=p[c][:], op=ALU.mult)
+        for c in halves:
+            nc.vector.tensor_tensor(out=t5[c][:], in0=t4[c][:], in1=spread(e[c][:]), op=ALU.mult)
+        for c in halves:
+            cols = slice(c * JH, (c + 1) * JH)
+            flat = y[c][:].rearrange("p g i -> p (g i)")
+            nc.vector.tensor_tensor(
+                out=flat, in0=old_sb[:, cols], in1=t5[c][:].rearrange("p g i -> p (g i)"), op=ALU.subtract
+            )
+            queue = nc.sync if c == 0 else nc.scalar
+            queue.dma_start(out=out[:, cols], in_=flat)

@@ -55,18 +55,21 @@ def tile_attend_cgroupvote_kernel(tc, tab_words, tab_scales, w1, steep, wo, dy, 
             return codes, scales
 
         w1_raw = load_rows(nc.sync, w1, "w1_raw")
-        steep_col = keep.tile([P, 1], F32, name="steep_col")
-        nc.sync.dma_start(out=steep_col[:], in_=steep)
         plane = keep.tile([P, T], U8, name="plane", align_bytes=64)
         nc.vector.memset(plane[:].bitcast(I32), 0)
         for q in range(4):
             nc.sync.dma_start(
-                out=plane[32 * q : 32 * q + 4, :].bitcast(I32), in_=tab_scales[0, 4 * q : 4 * q + 4, :].bitcast(I32)
+                out=plane[q:P:32, :].bitcast(I32), in_=tab_scales[0, q:16:4, :].bitcast(I32)
             )
         words = keep.tile([P, T], U32, name="words", align_bytes=64)
         nc.sync.dma_start(out=words[:].bitcast(I32), in_=tab_words[0].rearrange("p n t -> p (n t)").bitcast(I32))
+        steep_col = keep.tile([P, 1], F32, name="steep_col")
+        nc.sync.dma_start(out=steep_col[:], in_=steep)
         wo_raw = load_rows(nc.sync, wo, "wo_raw")
 
+        warm = keep.tile([P, 8], F32, name="warm")
+        nc.vector.memset(warm[:, 0:1], 0.0)
+        nc.scalar.activation(out=warm[:, 4:5], in_=warm[:, 0:1], func=ACT.Sigmoid)
 
         w1_grouped = interleave(w1_raw, "w1_grouped")
         dy_raw = load_rows(nc.sync, dy, "dy_raw")
@@ -146,6 +149,8 @@ def tile_attend_cgroupvote_kernel(tc, tab_words, tab_scales, w1, steep, wo, dy, 
                 out=t1[c][:], in0=h[c][:], scalar=steep_col[:], in1=spread(ms[c][:]), op0=ALU.mult, op1=ALU.subtract
             )
         for c in halves:
+            nc.vector.tensor_tensor(out=t4[c][:], in0=p[c][:], in1=spread(e[c][:]), op=ALU.mult)
+        for c in halves:
             nc.vector.scalar_tensor_tensor(
                 out=t2[c][:], in0=p[c][:], scalar=1.0, in1=t1[c][:], op0=ALU.subtract, op1=ALU.mult
             )
@@ -154,9 +159,7 @@ def tile_attend_cgroupvote_kernel(tc, tab_words, tab_scales, w1, steep, wo, dy, 
                 out=t3[c][:], in0=hh[c][:], scalar=1.0, in1=t2[c][:], op0=ALU.subtract, op1=ALU.add
             )
         for c in halves:
-            nc.vector.tensor_tensor(out=t4[c][:], in0=t3[c][:], in1=p[c][:], op=ALU.mult)
-        for c in halves:
-            nc.vector.tensor_tensor(out=t5[c][:], in0=t4[c][:], in1=spread(e[c][:]), op=ALU.mult)
+            nc.vector.tensor_tensor(out=t5[c][:], in0=t3[c][:], in1=t4[c][:], op=ALU.mult)
         for c in halves:
             cols = slice(c * JH, (c + 1) * JH)
             flat = y[c][:].rearrange("p g i -> p (g i)")

@@ -22,6 +22,10 @@ VOTE = J // G
 HALVES = 2
 JH = J // HALVES
 GH = G // HALVES
+SCALAR_GROUPS = 50
+FRONT = [(0, 32), (32, 64)]
+BACK = [(0, 16), (16, 32), (32, 48), (48, 64)]
+STORES = (32, 48, 64,)
 
 
 def tile_attend_cgroupvote_kernel(tc, tab_words, tab_scales, w1, steep, wo, dy, old, offs, out):
@@ -32,17 +36,18 @@ def tile_attend_cgroupvote_kernel(tc, tab_words, tab_scales, w1, steep, wo, dy, 
         psum = ctx.enter_context(tc.psum_pool(name="psum", bufs=1))
 
         offsets = keep.tile([P, J // 16], U16, name="offsets")
-        nc.sync.dma_start(offsets[:], offs)
 
         def load_rows(queue, rows, name):
             raw = stage.tile([P, PACK, rows.shape[1]], F32, name=name, tag="raw")
             queue.dma_start(out=raw[:], in_=rows.rearrange("(p t) w -> p t w", t=PACK))
             return raw
 
-        def interleave(raw, name):
+        def interleave(copy, raw, name):
             width = raw.shape[2]
             grouped = keep.tile([P, width, PACK], BF16, name=name, align_bytes=64)
-            nc.scalar.copy(out=grouped[:], in_=raw[:].rearrange("p t w -> p w t"))
+            copy(
+                out=grouped[:].rearrange("p (c i) t -> p c t i", i=4), in_=raw[:].rearrange("p t (c i) -> p c t i", i=4)
+            )
             return grouped
 
         def quantize(grouped, name):
@@ -55,6 +60,9 @@ def tile_attend_cgroupvote_kernel(tc, tab_words, tab_scales, w1, steep, wo, dy, 
             return codes, scales
 
         w1_raw = load_rows(nc.sync, w1, "w1_raw")
+        nc.sync.dma_start(offsets[:], offs)
+        steep_col = keep.tile([P, 1], F32, name="steep_col")
+        nc.scalar.dma_start(out=steep_col[:], in_=steep)
         plane = keep.tile([P, T], U8, name="plane", align_bytes=64)
         nc.vector.memset(plane[:].bitcast(I32), 0)
         for q in range(4):
@@ -63,15 +71,13 @@ def tile_attend_cgroupvote_kernel(tc, tab_words, tab_scales, w1, steep, wo, dy, 
             )
         words = keep.tile([P, T], U32, name="words", align_bytes=64)
         nc.sync.dma_start(out=words[:].bitcast(I32), in_=tab_words[0].rearrange("p n t -> p (n t)").bitcast(I32))
-        steep_col = keep.tile([P, 1], F32, name="steep_col")
-        nc.sync.dma_start(out=steep_col[:], in_=steep)
         wo_raw = load_rows(nc.sync, wo, "wo_raw")
 
         warm = keep.tile([P, 8], F32, name="warm")
         nc.vector.memset(warm[:, 0:1], 0.0)
         nc.scalar.activation(out=warm[:, 4:5], in_=warm[:, 0:1], func=ACT.Sigmoid)
 
-        w1_grouped = interleave(w1_raw, "w1_grouped")
+        w1_grouped = interleave(nc.scalar.copy, w1_raw, "w1_grouped")
         dy_raw = load_rows(nc.sync, dy, "dy_raw")
         w1_codes, w1_scales = quantize(w1_grouped, "w1")
 
@@ -82,43 +88,43 @@ def tile_attend_cgroupvote_kernel(tc, tab_words, tab_scales, w1, steep, wo, dy, 
         for c in range(HALVES):
             picked = keep.tile([P, JH], U32, name=f"picked_words{c}", align_bytes=64)
             nc.vector.tensor_copy(picked[:], words[:].indirect(offsets[:, c * (JH // 16) : (c + 1) * (JH // 16)]))
-            bank = psum.tile([P, JH], F32, name=f"a{c}")
-            nc.tensor.matmul_mx(
-                out=bank[:],
-                lhsT=w1_codes[:].bitcast(FP8X4),
-                lhsT_scale=w1_scales[:],
-                rhs=picked[:].bitcast(FP8X4),
-                rhs_scale=picked_scales[:, c * JH : (c + 1) * JH],
-                start=True,
-                stop=True,
-            )
-            a_banks.append(bank)
+            for lo, hi in FRONT:
+                if lo // GH != c:
+                    continue
+                bank = psum.tile([P, (hi - lo) * VOTE], F32, name=f"a{lo}")
+                nc.tensor.matmul_mx(
+                    out=bank[:],
+                    lhsT=w1_codes[:].bitcast(FP8X4),
+                    lhsT_scale=w1_scales[:],
+                    rhs=picked[:, lo * VOTE - c * JH : hi * VOTE - c * JH].bitcast(FP8X4),
+                    rhs_scale=picked_scales[:, lo * VOTE : hi * VOTE],
+                    start=True,
+                    stop=True,
+                )
+                a_banks.append(bank)
 
-        wo_grouped = interleave(wo_raw, "wo_grouped")
-        old_sb = stage.tile([P, J], F32, name="old_sb", tag="raw")
-        dy_grouped = interleave(dy_raw, "dy_grouped")
-        nc.sync.dma_start(out=old_sb[:], in_=old)
+        wo_grouped = interleave(nc.scalar.copy, wo_raw, "wo_grouped")
+        old_sb = stage.tile([P, G, VOTE], F32, name="old_sb", tag="raw")
+        dy_grouped = interleave(nc.vector.tensor_copy, dy_raw, "dy_grouped")
+        nc.sync.dma_start(out=old_sb[:], in_=old.rearrange("r (g i) -> r g i", i=VOTE))
 
         def wide(name):
-            return [keep.tile([P, GH, VOTE], F32, name=f"{name}{c}") for c in range(HALVES)]
+            return keep.tile([P, G, VOTE], F32, name=name)
 
         def narrow(name):
-            return [keep.tile([P, GH], F32, name=f"{name}{c}") for c in range(HALVES)]
+            return keep.tile([P, G], F32, name=name)
 
-        def spread(col):
-            return col.unsqueeze(2).to_broadcast([P, GH, VOTE])
+        def spread(col, lo, hi):
+            return col[:, lo:hi].unsqueeze(2).to_broadcast([P, hi - lo, VOTE])
 
         p, h, hh, ph = wide("p"), wide("h"), wide("hh"), wide("ph")
         z, rz, u, ms, e = narrow("z"), narrow("rz"), narrow("u"), narrow("ms"), narrow("e")
-        t1, t2, t3, t4, t5, y = wide("t1"), wide("t2"), wide("t3"), wide("t4"), wide("t5"), wide("y")
-        halves = range(HALVES)
+        t1, t2, t3, ep, t5, y = wide("t1"), wide("t2"), wide("t3"), wide("ep"), wide("t5"), wide("y")
 
-        for c in halves:
-            a = a_banks[c][:].rearrange("p (g i) -> p g i", i=VOTE)
-            nc.scalar.activation(out=p[c][:], in_=a, func=ACT.Sigmoid, scale=steep_col[:])
-            nc.scalar.activation(out=h[c][:], in_=a, func=ACT.Tanh)
-        for c in halves:
-            nc.scalar.activation(out=hh[c][:], in_=h[c][:], func=ACT.Square)
+        for bank, (lo, hi) in zip(a_banks, FRONT):
+            a = bank[:].rearrange("p (g i) -> p g i", i=VOTE)
+            nc.scalar.activation(out=p[:, lo:hi, :], in_=a, func=ACT.Sigmoid, scale=steep_col[:])
+            nc.scalar.activation(out=h[:, lo:hi, :], in_=a, func=ACT.Tanh)
 
         wo_codes, wo_scales = quantize(wo_grouped, "wo")
         dy_codes, dy_scales = quantize(dy_grouped, "dy")
@@ -133,38 +139,49 @@ def tile_attend_cgroupvote_kernel(tc, tab_words, tab_scales, w1, steep, wo, dy, 
             stop=True,
         )
 
-        for c in halves:
-            nc.vector.tensor_reduce(out=z[c][:], in_=p[c][:], axis=AXIS_X, op=ALU.add)
-            nc.vector.tensor_tensor(out=ph[c][:], in0=p[c][:], in1=h[c][:], op=ALU.mult)
-            nc.vector.reciprocal(out=rz[c][:], in_=z[c][:])
-            nc.vector.tensor_reduce(out=u[c][:], in_=ph[c][:], axis=AXIS_X, op=ALU.add)
-        for c in halves:
+        for lo, hi in FRONT:
+            nc.vector.tensor_reduce(out=z[:, lo:hi], in_=p[:, lo:hi, :], axis=AXIS_X, op=ALU.add)
+            nc.vector.tensor_tensor(out=ph[:, lo:hi, :], in0=p[:, lo:hi, :], in1=h[:, lo:hi, :], op=ALU.mult)
+            nc.vector.reciprocal(out=rz[:, lo:hi], in_=z[:, lo:hi])
+            nc.vector.tensor_reduce(out=u[:, lo:hi], in_=ph[:, lo:hi, :], axis=AXIS_X, op=ALU.add)
+            if hi % GH == 0:
+                half = slice(hi - GH, hi)
+                nc.vector.tensor_tensor(out=e[:, half], in0=c0[:, half], in1=rz[:, half], op=ALU.mult)
+                nc.vector.scalar_tensor_tensor(
+                    out=ms[:, half], in0=u[:, half], scalar=steep_col[:], in1=rz[:, half], op0=ALU.mult, op1=ALU.mult
+                )
+        for lo, hi in BACK:
             nc.vector.scalar_tensor_tensor(
-                out=ms[c][:], in0=u[c][:], scalar=steep_col[:], in1=rz[c][:], op0=ALU.mult, op1=ALU.mult
+                out=t1[:, lo:hi, :],
+                in0=h[:, lo:hi, :],
+                scalar=steep_col[:],
+                in1=spread(ms, lo, hi),
+                op0=ALU.mult,
+                op1=ALU.subtract,
             )
-        for c in halves:
-            nc.vector.tensor_tensor(out=e[c][:], in0=c0[:, c * GH : (c + 1) * GH], in1=rz[c][:], op=ALU.mult)
-        for c in halves:
+        for g in range(SCALAR_GROUPS):
+            nc.scalar.activation(out=ep[:, g, :], in_=p[:, g, :], func=ACT.Copy, scale=e[:, g : g + 1])
+            if g == GH - 1:
+                for c in range(HALVES):
+                    half = slice(c * GH, (c + 1) * GH)
+                    nc.scalar.activation(out=hh[:, half, :], in_=h[:, half, :], func=ACT.Square)
+        nc.vector.tensor_tensor(
+            out=ep[:, SCALAR_GROUPS:, :], in0=p[:, SCALAR_GROUPS:, :], in1=spread(e, SCALAR_GROUPS, G), op=ALU.mult
+        )
+        for lo, hi in BACK:
             nc.vector.scalar_tensor_tensor(
-                out=t1[c][:], in0=h[c][:], scalar=steep_col[:], in1=spread(ms[c][:]), op0=ALU.mult, op1=ALU.subtract
+                out=t2[:, lo:hi, :], in0=p[:, lo:hi, :], scalar=1.0, in1=t1[:, lo:hi, :], op0=ALU.subtract, op1=ALU.mult
             )
-        for c in halves:
-            nc.vector.tensor_tensor(out=t4[c][:], in0=p[c][:], in1=spread(e[c][:]), op=ALU.mult)
-        for c in halves:
+        for lo, hi in BACK:
             nc.vector.scalar_tensor_tensor(
-                out=t2[c][:], in0=p[c][:], scalar=1.0, in1=t1[c][:], op0=ALU.subtract, op1=ALU.mult
+                out=t3[:, lo:hi, :], in0=hh[:, lo:hi, :], scalar=1.0, in1=t2[:, lo:hi, :], op0=ALU.subtract, op1=ALU.add
             )
-        for c in halves:
-            nc.vector.scalar_tensor_tensor(
-                out=t3[c][:], in0=hh[c][:], scalar=1.0, in1=t2[c][:], op0=ALU.subtract, op1=ALU.add
-            )
-        for c in halves:
-            nc.vector.tensor_tensor(out=t5[c][:], in0=t3[c][:], in1=t4[c][:], op=ALU.mult)
-        for c in halves:
-            cols = slice(c * JH, (c + 1) * JH)
-            flat = y[c][:].rearrange("p g i -> p (g i)")
-            nc.vector.tensor_tensor(
-                out=flat, in0=old_sb[:, cols], in1=t5[c][:].rearrange("p g i -> p (g i)"), op=ALU.subtract
-            )
-            queue = nc.sync if c == 0 else nc.scalar
-            queue.dma_start(out=out[:, cols], in_=flat)
+        for lo, hi in BACK:
+            nc.vector.tensor_tensor(out=t5[:, lo:hi, :], in0=t3[:, lo:hi, :], in1=ep[:, lo:hi, :], op=ALU.mult)
+        done = 0
+        for lo, hi in BACK:
+            nc.vector.tensor_tensor(out=y[:, lo:hi, :], in0=old_sb[:, lo:hi, :], in1=t5[:, lo:hi, :], op=ALU.subtract)
+            if hi in STORES:
+                queue = nc.scalar if hi == G else nc.sync
+                queue.dma_start(out=out[:, done * VOTE : hi * VOTE], in_=y[:, done:hi, :].rearrange("p g i -> p (g i)"))
+                done = hi

from contextlib import ExitStack

import concourse.mybir as mybir

K, R, F, T, J, G = 512, 128, 512, 2048, 512, 64
FLOPS = 2 * K * R * J + 2 * F * R * G

F32 = mybir.dt.float32
BF16 = mybir.dt.bfloat16
I32 = mybir.dt.int32
U32 = mybir.dt.uint32
U16 = mybir.dt.uint16
U8 = mybir.dt.uint8
FP8X4 = mybir.dt.float8_e4m3fn_x4
ALU = mybir.AluOpType
ACT = mybir.ActivationFunctionType
AXIS_X = mybir.AxisListType.X

P = 128
PACK = 4
VOTE = J // G
HALVES = 2
JH = J // HALVES
GH = G // HALVES
SCALAR_GROUPS = 50
FRONT = [(0, 32), (32, 64)]
BACK = [(0, 16), (16, 32), (32, 48), (48, 64)]
STORES = (32, 48, 64,)


def tile_attend_cgroupvote_kernel(tc, tab_words, tab_scales, w1, steep, wo, dy, old, offs, out):
    nc = tc.nc
    with ExitStack() as ctx:
        keep = ctx.enter_context(tc.tile_pool(name="keep", bufs=1))
        stage = ctx.enter_context(tc.tile_pool(name="stage", bufs=4))
        psum = ctx.enter_context(tc.psum_pool(name="psum", bufs=1))

        offsets = keep.tile([P, J // 16], U16, name="offsets")

        def load_rows(queue, rows, name):
            raw = stage.tile([P, PACK, rows.shape[1]], F32, name=name, tag="raw")
            queue.dma_start(out=raw[:], in_=rows.rearrange("(p t) w -> p t w", t=PACK))
            return raw

        def interleave(copy, raw, name):
            width = raw.shape[2]
            grouped = keep.tile([P, width, PACK], BF16, name=name, align_bytes=64)
            copy(
                out=grouped[:].rearrange("p (c i) t -> p c t i", i=4), in_=raw[:].rearrange("p t (c i) -> p c t i", i=4)
            )
            return grouped

        def quantize(grouped, name):
            width = grouped.shape[1]
            codes = keep.tile([P, width], U32, name=name + "_codes", align_bytes=64)
            scales = keep.tile([P, width], U8, name=name + "_scales", align_bytes=64)
            nc.vector.quantize_mx(
                out=codes[:].bitcast(FP8X4), scales=scales[:], in_=grouped[:].rearrange("p w t -> p (w t)")
            )
            return codes, scales

        w1_raw = load_rows(nc.sync, w1, "w1_raw")
        nc.sync.dma_start(offsets[:], offs)
        steep_col = keep.tile([P, 1], F32, name="steep_col")
        nc.scalar.dma_start(out=steep_col[:], in_=steep)
        plane = keep.tile([P, T], U8, name="plane", align_bytes=64)
        nc.vector.memset(plane[:].bitcast(I32), 0)
        for q in range(4):
            nc.sync.dma_start(
                out=plane[q:P:32, :].bitcast(I32), in_=tab_scales[0, q:16:4, :].bitcast(I32)
            )
        words = keep.tile([P, T], U32, name="words", align_bytes=64)
        nc.sync.dma_start(out=words[:].bitcast(I32), in_=tab_words[0].rearrange("p n t -> p (n t)").bitcast(I32))
        wo_raw = load_rows(nc.sync, wo, "wo_raw")

        warm = keep.tile([P, 8], F32, name="warm")
        nc.vector.memset(warm[:, 0:1], 0.0)
        nc.scalar.activation(out=warm[:, 4:5], in_=warm[:, 0:1], func=ACT.Sigmoid)

        w1_grouped = interleave(nc.scalar.copy, w1_raw, "w1_grouped")
        dy_raw = load_rows(nc.sync, dy, "dy_raw")
        w1_codes, w1_scales = quantize(w1_grouped, "w1")

        picked_scales = keep.tile([P, J], U8, name="picked_scales", align_bytes=64)
        nc.vector.tensor_copy(picked_scales[:], plane[:].indirect(offsets[:]))

        a_banks = []
        for c in range(HALVES):
            picked = keep.tile([P, JH], U32, name=f"picked_words{c}", align_bytes=64)
            nc.vector.tensor_copy(picked[:], words[:].indirect(offsets[:, c * (JH // 16) : (c + 1) * (JH // 16)]))
            for lo, hi in FRONT:
                if lo // GH != c:
                    continue
                bank = psum.tile([P, (hi - lo) * VOTE], F32, name=f"a{lo}")
                nc.tensor.matmul_mx(
                    out=bank[:],
                    lhsT=w1_codes[:].bitcast(FP8X4),
                    lhsT_scale=w1_scales[:],
                    rhs=picked[:, lo * VOTE - c * JH : hi * VOTE - c * JH].bitcast(FP8X4),
                    rhs_scale=picked_scales[:, lo * VOTE : hi * VOTE],
                    start=True,
                    stop=True,
                )
                a_banks.append(bank)

        wo_grouped = interleave(nc.scalar.copy, wo_raw, "wo_grouped")
        old_sb = stage.tile([P, G, VOTE], F32, name="old_sb", tag="raw")
        dy_grouped = interleave(nc.vector.tensor_copy, dy_raw, "dy_grouped")
        nc.sync.dma_start(out=old_sb[:], in_=old.rearrange("r (g i) -> r g i", i=VOTE))

        def wide(name):
            return keep.tile([P, G, VOTE], F32, name=name)

        def narrow(name):
            return keep.tile([P, G], F32, name=name)

        def spread(col, lo, hi):
            return col[:, lo:hi].unsqueeze(2).to_broadcast([P, hi - lo, VOTE])

        p, h, hh, ph = wide("p"), wide("h"), wide("hh"), wide("ph")
        z, rz, u, ms, e = narrow("z"), narrow("rz"), narrow("u"), narrow("ms"), narrow("e")
        t1, t2, t3, ep, t5, y = wide("t1"), wide("t2"), wide("t3"), wide("ep"), wide("t5"), wide("y")

        for bank, (lo, hi) in zip(a_banks, FRONT):
            a = bank[:].rearrange("p (g i) -> p g i", i=VOTE)
            nc.scalar.activation(out=p[:, lo:hi, :], in_=a, func=ACT.Sigmoid, scale=steep_col[:])
            nc.scalar.activation(out=h[:, lo:hi, :], in_=a, func=ACT.Tanh)

        wo_codes, wo_scales = quantize(wo_grouped, "wo")
        dy_codes, dy_scales = quantize(dy_grouped, "dy")
        c0 = psum.tile([P, G], F32, name="c0")
        nc.tensor.matmul_mx(
            out=c0[:],
            lhsT=wo_codes[:].bitcast(FP8X4),
            lhsT_scale=wo_scales[:],
            rhs=dy_codes[:].bitcast(FP8X4),
            rhs_scale=dy_scales[:],
            start=True,
            stop=True,
        )

        for lo, hi in FRONT:
            nc.vector.tensor_reduce(out=z[:, lo:hi], in_=p[:, lo:hi, :], axis=AXIS_X, op=ALU.add)
            nc.vector.tensor_tensor(out=ph[:, lo:hi, :], in0=p[:, lo:hi, :], in1=h[:, lo:hi, :], op=ALU.mult)
            nc.vector.reciprocal(out=rz[:, lo:hi], in_=z[:, lo:hi])
            nc.vector.tensor_reduce(out=u[:, lo:hi], in_=ph[:, lo:hi, :], axis=AXIS_X, op=ALU.add)
            if hi % GH == 0:
                half = slice(hi - GH, hi)
                nc.vector.tensor_tensor(out=e[:, half], in0=c0[:, half], in1=rz[:, half], op=ALU.mult)
                nc.vector.scalar_tensor_tensor(
                    out=ms[:, half], in0=u[:, half], scalar=steep_col[:], in1=rz[:, half], op0=ALU.mult, op1=ALU.mult
                )
        for lo, hi in BACK:
            nc.vector.scalar_tensor_tensor(
                out=t1[:, lo:hi, :],
                in0=h[:, lo:hi, :],
                scalar=steep_col[:],
                in1=spread(ms, lo, hi),
                op0=ALU.mult,
                op1=ALU.subtract,
            )
        for g in range(SCALAR_GROUPS):
            nc.scalar.activation(out=ep[:, g, :], in_=p[:, g, :], func=ACT.Copy, scale=e[:, g : g + 1])
            if g == GH - 1:
                for c in range(HALVES):
                    half = slice(c * GH, (c + 1) * GH)
                    nc.scalar.activation(out=hh[:, half, :], in_=h[:, half, :], func=ACT.Square)
        nc.vector.tensor_tensor(
            out=ep[:, SCALAR_GROUPS:, :], in0=p[:, SCALAR_GROUPS:, :], in1=spread(e, SCALAR_GROUPS, G), op=ALU.mult
        )
        for lo, hi in BACK:
            nc.vector.scalar_tensor_tensor(
                out=t2[:, lo:hi, :], in0=p[:, lo:hi, :], scalar=1.0, in1=t1[:, lo:hi, :], op0=ALU.subtract, op1=ALU.mult
            )
        for lo, hi in BACK:
            nc.vector.scalar_tensor_tensor(
                out=t3[:, lo:hi, :], in0=hh[:, lo:hi, :], scalar=1.0, in1=t2[:, lo:hi, :], op0=ALU.subtract, op1=ALU.add
            )
        for lo, hi in BACK:
            nc.vector.tensor_tensor(out=t5[:, lo:hi, :], in0=t3[:, lo:hi, :], in1=ep[:, lo:hi, :], op=ALU.mult)
        done = 0
        for lo, hi in BACK:
            nc.vector.tensor_tensor(out=y[:, lo:hi, :], in0=old_sb[:, lo:hi, :], in1=t5[:, lo:hi, :], op=ALU.subtract)
            if hi in STORES:
                queue = nc.scalar if hi == G else nc.sync
                queue.dma_start(out=out[:, done * VOTE : hi * VOTE], in_=y[:, done:hi, :].rearrange("p g i -> p (g i)"))
                done = hi
